import numpy as np
import ml_dtypes


def mxq(x, axis, fmt="e4m3"):
    dtype, down = {"e4m3": (ml_dtypes.float8_e4m3fn, 7), "e5m2": (ml_dtypes.float8_e5m2, 14)}[fmt]
    v = np.moveaxis(np.asarray(x, np.float32).astype(ml_dtypes.bfloat16).astype(np.float64), axis, -1)
    blocks = v.reshape(v.shape[:-1] + (-1, 32))
    amax = np.abs(blocks).max(-1, keepdims=True)
    byte = np.maximum(np.where(amax > 0, np.frexp(amax)[1] - 1 + 127, 0) - down, 1)
    scale = np.exp2(byte - 127.0)
    codes = (blocks / scale).astype(np.float32).astype(dtype).astype(np.float64)
    return np.moveaxis((codes * scale).reshape(v.shape), -1, axis)


WIDE = False


def mx_kscale(k):
    if not WIDE:
        return np.ones(k)
    levels = np.array([10, -10, 5, -5, 0])
    if k % 512:
        return np.exp2(np.random.permutation(np.resize(levels, k // 32))).repeat(32)
    a = np.empty((k // 512, 16))
    for p in range(k // 512):
        a[p, :8] = np.random.permutation(np.resize(levels, 8))
        for g in range(8):
            far = levels[np.abs(levels - a[p, g]) >= 10]
            a[p, g + 8] = far[np.random.randint(len(far))]
    return np.exp2(a.ravel()).repeat(32)


BF16 = ml_dtypes.bfloat16


def bf(x):
    return np.asarray(x, np.float32).astype(BF16)


def f64(x):
    return np.asarray(x).astype(np.float64)


E2M1 = np.array([0.0, 0.5, 1.0, 1.5, 2.0, 3.0, 4.0, 6.0, -0.0, -0.5, -1.0, -1.5, -2.0, -3.0, -4.0, -6.0])


def pack_weight(w, fmt):
    k, n = w.shape
    w = f64(bf(w)).reshape(k // 32, 32, n)
    amax = np.abs(w).max(1)
    if fmt == "e4m3":
        byte = np.frexp(amax)[1] - 1 + 127 - 7
    else:
        mant, ex = np.frexp(amax / 6.0)
        byte = np.where(mant > 0.5, ex, ex - 1) + 127
    byte = np.clip(np.where(amax > 0, byte, 1), 1, 254)
    scaled = (w * np.exp2(127.0 - byte)[:, None, :]).reshape(k, n).astype(np.float32)
    by_word = np.ascontiguousarray(scaled.reshape(k // 512, 128, 4, n).transpose(0, 1, 3, 2))
    if fmt == "e4m3":
        words = by_word.astype(ml_dtypes.float8_e4m3fn).view(np.uint8)
    else:
        c = by_word.astype(ml_dtypes.float4_e2m1fn).view(np.uint8) & 0xF
        words = c[..., 0::2] | (c[..., 1::2] << 4)
    return np.ascontiguousarray(words), np.ascontiguousarray(byte.astype(np.uint8).reshape(k // 512, 16, n))


def unpack_weight(words, scales, fmt):
    g, p, n, _ = words.shape
    if fmt == "e4m3":
        vals = np.ascontiguousarray(words).view(ml_dtypes.float8_e4m3fn).astype(np.float64)
    else:
        nib = np.empty((g, p, n, 4), np.uint8)
        nib[..., 0::2] = words & 0xF
        nib[..., 1::2] = words >> 4
        vals = E2M1[nib]
    vals = vals * np.repeat(np.exp2(scales.astype(np.float64) - 127.0), 8, axis=1)[..., None]
    return vals.transpose(0, 1, 3, 2).reshape(g * 512, n)
def pack4(w):
    words, scales = pack_weight(w, "e2m1")
    return words.reshape(words.shape[0], 128, -1), scales


def unpack4(words, scales):
    return unpack_weight(words.reshape(words.shape[0], 128, -1, 2), scales, "e2m1")


V, C, A, R = 1024, 1024, 2048, 1024


def setup_inputs():
    s = mx_kscale(C)
    t = mx_kscale(A)
    sig_words, sig_scales = pack4(np.random.standard_normal((C, V)) * s[:, None])
    dic_words, dic_scales = pack4(np.random.standard_normal((C, A)) / np.sqrt(C) / s[:, None])
    tab_words, tab_scales = pack_weight(np.random.standard_normal((A, R)) / np.sqrt(A) / t[:, None], "e4m3")
    return {"sig_words": sig_words, "sig_scales": sig_scales,
            "dic_words": dic_words, "dic_scales": dic_scales,
            "tab_words": tab_words, "tab_scales": tab_scales,
            "inv_norm2": bf((1 + 0.1 * np.random.standard_normal(A)) * t),
            "inv_energy": bf(1 + 0.1 * np.random.standard_normal(V)),
            "base": bf(0.3 * np.random.standard_normal(R))}


def reference(sig_words, sig_scales, dic_words, dic_scales, tab_words, tab_scales, inv_norm2, inv_energy, base):
    x = unpack4(sig_words, sig_scales)
    d = unpack4(dic_words, dic_scales)
    m = unpack_weight(tab_words, tab_scales, "e4m3")
    c = x.T @ d
    e = c * c * f64(inv_norm2)
    maps = mxq(e, 1, "e4m3") @ m
    return maps * f64(inv_energy)[:, None] + f64(base)

@@ -1,0 +1,259 @@
+from contextlib import ExitStack
+
+import concourse.mybir as mybir
+
+V, C, A, R = 1024, 1024, 2048, 1024
+FLOPS = 2 * V * C * A + 2 * V * A * R
+
+F32 = mybir.dt.float32
+BF16 = mybir.dt.bfloat16
+I32 = mybir.dt.int32
+U32 = mybir.dt.uint32
+U8 = mybir.dt.uint8
+FP4X4 = mybir.dt.float4_e2m1fn_x4
+FP8X4 = mybir.dt.float8_e4m3fn_x4
+ACT = mybir.ActivationFunctionType
+ALU = mybir.AluOpType
+
+P = 128
+PACK = 4
+K_PASS = P * PACK
+N = 512
+C_PASSES = C // K_PASS
+GROUPS = A // K_PASS
+HALVES = V // N
+R_HALVES = R // N
+PART = N // 2
+QUADS = 4
+
+
+def tile_fingerprint_squared_match_maps_s4_kernel(
+    tc, sig_words, sig_scales, dic_words, dic_scales, tab_words, tab_scales, inv_norm2, inv_energy, base, out
+):
+    nc = tc.nc
+    with ExitStack() as ctx:
+        keep = ctx.enter_context(tc.tile_pool(name="keep", bufs=1))
+        work = ctx.enter_context(tc.tile_pool(name="work", bufs=1))
+        psum = ctx.enter_context(tc.psum_pool(name="psum", bufs=8))
+        ctx.enter_context(tc.manual_schedule())
+
+        def kept(shape, dtype, name):
+            return keep.tile(shape, dtype, name=name, align_bytes=64)
+
+        x_words = [kept([P, C_PASSES, 2 * N], U8, "x_words%d" % h) for h in range(HALVES)]
+        x_scales = [kept([P, C_PASSES, N], U8, "x_scales%d" % h) for h in range(HALVES)]
+        d_raw = [kept([P, C_PASSES, 2 * K_PASS], U8, "d_raw%d" % g) for g in range(GROUPS)]
+        d_raw_scales = [kept([P, C_PASSES, 2 * K_PASS], U8, "d_raw_scales%d" % j) for j in range(GROUPS // 2)]
+        m_words = [kept([P, R], U32, "m_words%d" % g) for g in range(GROUPS)]
+        m_scales = kept([P, R], U8, "m_scales")
+        norm_bf = kept([P, GROUPS, PACK], BF16, "norm_bf")
+        norm = kept([P, GROUPS, PACK], F32, "norm")
+        energy = kept([P, HALVES, PACK], BF16, "energy")
+        base_all = kept([P, R], BF16, "base_all")
+
+        def load_words(queue, tile, src, cols):
+            queue.dma_start(
+                out=tile[:].bitcast(I32),
+                in_=src.rearrange("c p n -> p c n")[:, :, cols].bitcast(I32),
+            )
+
+        def load_scale_rows(queue, tile, src, cols, q):
+            queue.dma_start(
+                out=tile[32 * q : 32 * q + 4, :, :].bitcast(I32),
+                in_=src.rearrange("c r n -> r c n")[4 * q : 4 * q + 4, :, cols].bitcast(I32),
+            )
+
+        def span(j, width):
+            return slice(j * width, (j + 1) * width)
+
+        nc.gpsimd.memset(x_scales[0][:].bitcast(I32), 0)
+        nc.vector.memset(d_raw_scales[0][:].bitcast(I32), 0)
+        load_words(nc.scalar, d_raw[0], dic_words, span(0, 2 * K_PASS))
+        load_words(nc.scalar, x_words[0], sig_words, span(0, 2 * N))
+        for q in range(QUADS):
+            load_scale_rows(nc.sync, d_raw_scales[0], dic_scales, span(0, 2 * K_PASS), q)
+        for q in range(QUADS):
+            load_scale_rows(nc.sync if q < 2 else nc.gpsimd, x_scales[0], sig_scales, span(0, N), q)
+        nc.vector.memset(d_raw_scales[1][:].bitcast(I32), 0)
+        nc.vector.memset(x_scales[1][:].bitcast(I32), 0)
+        nc.vector.memset(m_scales[:].bitcast(I32), 0)
+        for g in range(1, GROUPS):
+            load_words(nc.sync, d_raw[g], dic_words, span(g, 2 * K_PASS))
+        for q in range(QUADS):
+            load_scale_rows(nc.sync, d_raw_scales[1], dic_scales, span(1, 2 * K_PASS), q)
+        nc.sync.dma_start(out=norm_bf[:], in_=inv_norm2.rearrange("(g p t) -> p g t", p=P, t=PACK))
+        load_words(nc.sync, x_words[1], sig_words, span(1, 2 * N))
+        for q in range(QUADS):
+            load_scale_rows(nc.sync, x_scales[1], sig_scales, span(1, N), q)
+        for q in range(QUADS):
+            nc.sync.dma_start(
+                out=m_scales[32 * q : 32 * q + 16, :].bitcast(I32),
+                in_=tab_scales[:, 4 * q : 4 * q + 4, :].bitcast(I32),
+            )
+        for g in range(GROUPS):
+            nc.sync.dma_start(
+                out=m_words[g][:].bitcast(I32),
+                in_=tab_words[g].rearrange("p n t -> p (n t)").bitcast(I32),
+            )
+        nc.sync.dma_start(out=energy[:], in_=inv_energy.rearrange("(h m i) -> m h i", m=P, i=PACK))
+        nc.sync.dma_start(out=base_all[:], in_=base.partition_broadcast(P))
+        nc.gpsimd.tensor_copy(out=norm[:], in_=norm_bf[:])
+
+        d_words = {}
+        d_scales = {}
+
+        def sort_atoms(g, t0, nt):
+            words = kept([P, C_PASSES, nt, 2 * P], U8, "d_words%d_%d" % (g, t0))
+            scales = kept([P, C_PASSES, nt, P], U8, "d_scales%d_%d" % (g, t0))
+            nc.vector.tensor_copy(
+                out=words[:].rearrange("p c t (m b) -> p c t m b", b=2),
+                in_=d_raw[g][:].rearrange("p c (m t b) -> p c t m b", t=PACK, b=2)[:, :, t0 : t0 + nt, :, :],
+            )
+            raw = d_raw_scales[g // 2][:, :, span(g % 2, K_PASS)]
+            nc.vector.tensor_copy(
+                out=scales[:],
+                in_=raw.rearrange("p c (m t) -> p c t m", t=PACK)[:, :, t0 : t0 + nt, :],
+            )
+            for j in range(nt):
+                d_words[g, t0 + j] = words[:, :, j, :]
+                d_scales[g, t0 + j] = scales[:, :, j, :]
+
+        squares = {}
+
+        def correlate(g, h):
+            sq = work.tile([P, PACK, N], F32, tag="squares", bufs=8)
+            for t in range(PACK):
+                bank = psum.tile([P, N], F32, tag="bank")
+                for c in range(C_PASSES):
+                    nc.tensor.matmul_mx(
+                        out=bank[:],
+                        lhsT=d_words[g, t][:, c, :].bitcast(FP4X4),
+                        lhsT_scale=d_scales[g, t][:, c, :],
+                        rhs=x_words[h][:, c, :].bitcast(FP4X4),
+                        rhs_scale=x_scales[h][:, c, :],
+                        start=(c == 0),
+                        stop=(c == C_PASSES - 1),
+                    )
+                nc.scalar.activation(
+                    out=sq[:, t, :].rearrange("p (i m) -> p i m", i=PACK),
+                    in_=bank[:].rearrange("p (m i) -> p i m", i=PACK),
+                    func=ACT.Square,
+                )
+            squares[g, h] = sq
+
+        e_words = {}
+        e_scales = {}
+
+        def quantize(g, h, grouped):
+            for u in range(2):
+                words = kept([P, PART], U32, "e_words%d_%d_%d" % (g, h, u))
+                scales = kept([P, PART], U8, "e_scales%d_%d_%d" % (g, h, u))
+                nc.vector.quantize_mx(
+                    out=words[:].bitcast(FP8X4),
+                    scales=scales[:],
+                    in_=grouped[u][:].rearrange("p j t -> p (j t)"),
+                )
+                e_words[g, h, u] = words
+                e_scales[g, h, u] = scales
+
+        def weigh_on_vector(g, h):
+            grouped = []
+            for u in range(2):
+                part = work.tile([P, PART, PACK], BF16, tag="grouped", bufs=4, align_bytes=64)
+                nc.vector.tensor_tensor(
+                    out=part[:].rearrange("p (j i) t -> p j t i", i=2),
+                    in0=squares[g, h][:, :, span(u, PART)].rearrange("p t (j i) -> p j t i", i=2),
+                    in1=norm[:, g, :].unsqueeze(1).unsqueeze(3).to_broadcast([P, PART // 2, PACK, 2]),
+                    op=ALU.mult,
+                )
+                grouped.append(part)
+            quantize(g, h, grouped)
+
+        weighted = {}
+
+        def weigh_on_scalar(g, h):
+            rows = work.tile([P, PACK, N], BF16, tag="weighted", bufs=3, align_bytes=64)
+            for t in range(PACK):
+                nc.scalar.activation(
+                    out=rows[:, t, :], in_=squares[g, h][:, t, :], func=ACT.Copy, scale=norm[:, g, t : t + 1]
+                )
+            weighted[g, h] = rows
+
+        def interleave(g, h):
+            grouped = []
+            for u in range(2):
+                part = work.tile([P, PART, PACK], BF16, tag="grouped", bufs=4, align_bytes=64)
+                nc.vector.tensor_copy(
+                    out=part[:].rearrange("p (j i) t -> p j t i", i=4),
+                    in_=weighted[g, h][:, :, span(u, PART)].rearrange("p t (j i) -> p j t i", i=4),
+                )
+                grouped.append(part)
+            quantize(g, h, grouped)
+
+        sums = {}
+
+        def map_passes(h, i, r, groups):
+            if (h, i, r) not in sums:
+                bank = psum.tile([P, N], F32, tag="bank")
+                sums[h, i, r] = bank
+            cols = span(i % 2, P)
+            for g in groups:
+                nc.tensor.matmul_mx(
+                    out=sums[h, i, r][:],
+                    lhsT=e_words[g, h, i // 2][:, cols].bitcast(FP8X4),
+                    lhsT_scale=e_scales[g, h, i // 2][:, cols],
+                    rhs=m_words[g][:, span(r, N)].bitcast(FP8X4),
+                    rhs_scale=m_scales[4 * g :, span(r, N)],
+                    start=(g == 0),
+                    stop=(g == GROUPS - 1),
+                )
+
+        out_rows = out.rearrange("(h m i) r -> h i m r", m=P, i=PACK)
+
+        def finish(h, i, r):
+            res = work.tile([P, N], F32, tag="result", bufs=6)
+            nc.vector.scalar_tensor_tensor(
+                out=res[:],
+                in0=sums[h, i, r][:],
+                scalar=energy[:, h, i : i + 1],
+                in1=base_all[:, span(r, N)],
+                op0=ALU.mult,
+                op1=ALU.add,
+            )
+            nc.sync.dma_start(out=out_rows[h, i, :, span(r, N)], in_=res[:])
+
+        for t in range(PACK):
+            sort_atoms(0, t, 1)
+        correlate(0, 0)
+        for g in range(1, GROUPS):
+            sort_atoms(g, 0, PACK)
+            correlate(g, 0)
+        for g in range(GROUPS):
+            correlate(g, 1)
+            weigh_on_vector(g, 0)
+        weigh_on_vector(0, 1)
+        for g in range(1, GROUPS):
+            weigh_on_scalar(g, 1)
+
+        tiles = [(i, r) for i in range(PACK) for r in range(R_HALVES)]
+        everything = list(range(GROUPS))
+        for i, r in tiles:
+            map_passes(0, i, r, everything)
+        finish(0, *tiles[0])
+        interleave(1, 1)
+        finish(0, *tiles[1])
+        finish(0, *tiles[2])
+        interleave(2, 1)
+        finish(0, *tiles[3])
+        interleave(3, 1)
+        for i, r in tiles[:2]:
+            map_passes(1, i, r, everything[:-1])
+        for i, r in tiles[:2]:
+            map_passes(1, i, r, everything[-1:])
+        for i, r in tiles[2:4]:
+            map_passes(1, i, r, everything)
+        for i, r in tiles[4:]:
+            finish(0, i, r)
+            map_passes(1, i, r, everything)
+        for i, r in tiles:
+            finish(1, i, r)

@@ -192,35 +192,37 @@ def tile_fingerprint_squared_match_maps_s4_kernel(
 
         sums = {}
 
-        def map_passes(h, i, r, groups):
-            if (h, i, r) not in sums:
-                bank = psum.tile([P, N], F32, tag="bank")
-                sums[h, i, r] = bank
-            cols = span(i % 2, P)
+        def map_passes(h, i, cols, groups):
+            key = (h, i, cols.start)
+            width = cols.stop - cols.start
+            if key not in sums:
+                bank = psum.tile([P, width], F32, tag="bank")
+                sums[key] = bank
+            voxels = span(i % 2, P)
             for g in groups:
                 nc.tensor.matmul_mx(
-                    out=sums[h, i, r][:],
-                    lhsT=e_words[g, h, i // 2][:, cols].bitcast(FP8X4),
-                    lhsT_scale=e_scales[g, h, i // 2][:, cols],
-                    rhs=m_words[g][:, span(r, N)].bitcast(FP8X4),
-                    rhs_scale=m_scales[4 * g :, span(r, N)],
+                    out=sums[key][:],
+                    lhsT=e_words[g, h, i // 2][:, voxels].bitcast(FP8X4),
+                    lhsT_scale=e_scales[g, h, i // 2][:, voxels],
+                    rhs=m_words[g][:, cols].bitcast(FP8X4),
+                    rhs_scale=m_scales[4 * g :, cols],
                     start=(g == 0),
                     stop=(g == GROUPS - 1),
                 )
 
         out_rows = out.rearrange("(h m i) r -> h i m r", m=P, i=PACK)
 
-        def finish(h, i, r):
-            res = work.tile([P, N], F32, tag="result", bufs=6)
+        def finish(h, i, cols):
+            res = work.tile([P, cols.stop - cols.start], F32, tag="result", bufs=8)
             nc.vector.scalar_tensor_tensor(
                 out=res[:],
-                in0=sums[h, i, r][:],
+                in0=sums[h, i, cols.start][:],
                 scalar=energy[:, h, i : i + 1],
-                in1=base_all[:, span(r, N)],
+                in1=base_all[:, cols],
                 op0=ALU.mult,
                 op1=ALU.add,
             )
-            nc.sync.dma_start(out=out_rows[h, i, :, span(r, N)], in_=res[:])
+            nc.sync.dma_start(out=out_rows[h, i, :, cols], in_=res[:])
 
         for t in range(PACK):
             sort_atoms(0, t, 1)
@@ -235,25 +237,31 @@ def tile_fingerprint_squared_match_maps_s4_kernel(
         for g in range(1, GROUPS):
             weigh_on_scalar(g, 1)
 
-        tiles = [(i, r) for i in range(PACK) for r in range(R_HALVES)]
+        tiles = [(i, span(r, N)) for i in range(PACK) for r in range(R_HALVES)]
+        early, late = tiles[:4], tiles[4:]
         everything = list(range(GROUPS))
-        for i, r in tiles:
-            map_passes(0, i, r, everything)
-        finish(0, *tiles[0])
+        for g in everything:
+            for i, cols in early:
+                map_passes(0, i, cols, [g])
+        for i, cols in late:
+            map_passes(0, i, cols, everything)
         interleave(1, 1)
-        finish(0, *tiles[1])
-        finish(0, *tiles[2])
+        for i, cols in early[:2]:
+            finish(0, i, cols)
         interleave(2, 1)
-        finish(0, *tiles[3])
+        for i, cols in early[2:]:
+            finish(0, i, cols)
         interleave(3, 1)
-        for i, r in tiles[:2]:
-            map_passes(1, i, r, everything[:-1])
-        for i, r in tiles[:2]:
-            map_passes(1, i, r, everything[-1:])
-        for i, r in tiles[2:4]:
-            map_passes(1, i, r, everything)
-        for i, r in tiles[4:]:
-            finish(0, i, r)
-            map_passes(1, i, r, everything)
-        for i, r in tiles:
-            finish(1, i, r)
+        for i, cols in early:
+            map_passes(1, i, cols, everything[:-1])
+        for i, cols in early:
+            map_passes(1, i, cols, everything[-1:])
+        for i, cols in late:
+            finish(0, i, cols)
+        last = late[:-1] + [(PACK - 1, span(j, PART)) for j in (2, 3)]
+        for i, cols in last[:-1]:
+            map_passes(1, i, cols, everything)
+        finish(1, *early[0])
+        map_passes(1, *last[-1], everything)
+        for i, cols in early[1:] + last:
+            finish(1, i, cols)

from contextlib import ExitStack

import concourse.mybir as mybir

V, C, A, R = 1024, 1024, 2048, 1024
FLOPS = 2 * V * C * A + 2 * V * A * R

F32 = mybir.dt.float32
BF16 = mybir.dt.bfloat16
I32 = mybir.dt.int32
U32 = mybir.dt.uint32
U8 = mybir.dt.uint8
FP4X4 = mybir.dt.float4_e2m1fn_x4
FP8X4 = mybir.dt.float8_e4m3fn_x4
ACT = mybir.ActivationFunctionType
ALU = mybir.AluOpType

P = 128
PACK = 4
K_PASS = P * PACK
N = 512
C_PASSES = C // K_PASS
GROUPS = A // K_PASS
HALVES = V // N
R_HALVES = R // N
PART = N // 2
QUADS = 4


def tile_fingerprint_squared_match_maps_s4_kernel(
    tc, sig_words, sig_scales, dic_words, dic_scales, tab_words, tab_scales, inv_norm2, inv_energy, base, out
):
    nc = tc.nc
    with ExitStack() as ctx:
        keep = ctx.enter_context(tc.tile_pool(name="keep", bufs=1))
        work = ctx.enter_context(tc.tile_pool(name="work", bufs=1))
        psum = ctx.enter_context(tc.psum_pool(name="psum", bufs=8))
        ctx.enter_context(tc.manual_schedule())

        def kept(shape, dtype, name):
            return keep.tile(shape, dtype, name=name, align_bytes=64)

        x_words = [kept([P, C_PASSES, 2 * N], U8, "x_words%d" % h) for h in range(HALVES)]
        x_scales = [kept([P, C_PASSES, N], U8, "x_scales%d" % h) for h in range(HALVES)]
        d_raw = [kept([P, C_PASSES, 2 * K_PASS], U8, "d_raw%d" % g) for g in range(GROUPS)]
        d_raw_scales = [kept([P, C_PASSES, 2 * K_PASS], U8, "d_raw_scales%d" % j) for j in range(GROUPS // 2)]
        m_words = [kept([P, R], U32, "m_words%d" % g) for g in range(GROUPS)]
        m_scales = kept([P, R], U8, "m_scales")
        norm_bf = kept([P, GROUPS, PACK], BF16, "norm_bf")
        norm = kept([P, GROUPS, PACK], F32, "norm")
        energy = kept([P, HALVES, PACK], BF16, "energy")
        base_all = kept([P, R], BF16, "base_all")

        def load_words(queue, tile, src, cols):
            queue.dma_start(
                out=tile[:].bitcast(I32),
                in_=src.rearrange("c p n -> p c n")[:, :, cols].bitcast(I32),
            )

        def load_scale_rows(queue, tile, src, cols, q):
            queue.dma_start(
                out=tile[32 * q : 32 * q + 4, :, :].bitcast(I32),
                in_=src.rearrange("c r n -> r c n")[4 * q : 4 * q + 4, :, cols].bitcast(I32),
            )

        def span(j, width):
            return slice(j * width, (j + 1) * width)

        nc.gpsimd.memset(x_scales[0][:].bitcast(I32), 0)
        nc.vector.memset(d_raw_scales[0][:].bitcast(I32), 0)
        load_words(nc.scalar, d_raw[0], dic_words, span(0, 2 * K_PASS))
        load_words(nc.scalar, x_words[0], sig_words, span(0, 2 * N))
        for q in range(QUADS):
            load_scale_rows(nc.sync, d_raw_scales[0], dic_scales, span(0, 2 * K_PASS), q)
        for q in range(QUADS):
            load_scale_rows(nc.sync if q < 2 else nc.gpsimd, x_scales[0], sig_scales, span(0, N), q)
        nc.vector.memset(d_raw_scales[1][:].bitcast(I32), 0)
        nc.vector.memset(x_scales[1][:].bitcast(I32), 0)
        nc.vector.memset(m_scales[:].bitcast(I32), 0)
        for g in range(1, GROUPS):
            load_words(nc.sync, d_raw[g], dic_words, span(g, 2 * K_PASS))
        for q in range(QUADS):
            load_scale_rows(nc.sync, d_raw_scales[1], dic_scales, span(1, 2 * K_PASS), q)
        nc.sync.dma_start(out=norm_bf[:], in_=inv_norm2.rearrange("(g p t) -> p g t", p=P, t=PACK))
        load_words(nc.sync, x_words[1], sig_words, span(1, 2 * N))
        for q in range(QUADS):
            load_scale_rows(nc.sync, x_scales[1], sig_scales, span(1, N), q)
        for q in range(QUADS):
            nc.sync.dma_start(
                out=m_scales[32 * q : 32 * q + 16, :].bitcast(I32),
                in_=tab_scales[:, 4 * q : 4 * q + 4, :].bitcast(I32),
            )
        for g in range(GROUPS):
            nc.sync.dma_start(
                out=m_words[g][:].bitcast(I32),
                in_=tab_words[g].rearrange("p n t -> p (n t)").bitcast(I32),
            )
        nc.sync.dma_start(out=energy[:], in_=inv_energy.rearrange("(h m i) -> m h i", m=P, i=PACK))
        nc.sync.dma_start(out=base_all[:], in_=base.partition_broadcast(P))
        nc.gpsimd.tensor_copy(out=norm[:], in_=norm_bf[:])

        d_words = {}
        d_scales = {}

        def sort_atoms(g, t0, nt):
            words = kept([P, C_PASSES, nt, 2 * P], U8, "d_words%d_%d" % (g, t0))
            scales = kept([P, C_PASSES, nt, P], U8, "d_scales%d_%d" % (g, t0))
            nc.vector.tensor_copy(
                out=words[:].rearrange("p c t (m b) -> p c t m b", b=2),
                in_=d_raw[g][:].rearrange("p c (m t b) -> p c t m b", t=PACK, b=2)[:, :, t0 : t0 + nt, :, :],
            )
            raw = d_raw_scales[g // 2][:, :, span(g % 2, K_PASS)]
            nc.vector.tensor_copy(
                out=scales[:],
                in_=raw.rearrange("p c (m t) -> p c t m", t=PACK)[:, :, t0 : t0 + nt, :],
            )
            for j in range(nt):
                d_words[g, t0 + j] = words[:, :, j, :]
                d_scales[g, t0 + j] = scales[:, :, j, :]

        squares = {}

        def correlate(g, h):
            sq = work.tile([P, PACK, N], F32, tag="squares", bufs=8)
            for t in range(PACK):
                bank = psum.tile([P, N], F32, tag="bank")
                for c in range(C_PASSES):
                    nc.tensor.matmul_mx(
                        out=bank[:],
                        lhsT=d_words[g, t][:, c, :].bitcast(FP4X4),
                        lhsT_scale=d_scales[g, t][:, c, :],
                        rhs=x_words[h][:, c, :].bitcast(FP4X4),
                        rhs_scale=x_scales[h][:, c, :],
                        start=(c == 0),
                        stop=(c == C_PASSES - 1),
                    )
                nc.scalar.activation(
                    out=sq[:, t, :].rearrange("p (i m) -> p i m", i=PACK),
                    in_=bank[:].rearrange("p (m i) -> p i m", i=PACK),
                    func=ACT.Square,
                )
            squares[g, h] = sq

        e_words = {}
        e_scales = {}

        def quantize(g, h, grouped):
            for u in range(2):
                words = kept([P, PART], U32, "e_words%d_%d_%d" % (g, h, u))
                scales = kept([P, PART], U8, "e_scales%d_%d_%d" % (g, h, u))
                nc.vector.quantize_mx(
                    out=words[:].bitcast(FP8X4),
                    scales=scales[:],
                    in_=grouped[u][:].rearrange("p j t -> p (j t)"),
                )
                e_words[g, h, u] = words
                e_scales[g, h, u] = scales

        def weigh_on_vector(g, h):
            grouped = []
            for u in range(2):
                part = work.tile([P, PART, PACK], BF16, tag="grouped", bufs=4, align_bytes=64)
                nc.vector.tensor_tensor(
                    out=part[:].rearrange("p (j i) t -> p j t i", i=2),
                    in0=squares[g, h][:, :, span(u, PART)].rearrange("p t (j i) -> p j t i", i=2),
                    in1=norm[:, g, :].unsqueeze(1).unsqueeze(3).to_broadcast([P, PART // 2, PACK, 2]),
                    op=ALU.mult,
                )
                grouped.append(part)
            quantize(g, h, grouped)

        weighted = {}

        def weigh_on_scalar(g, h):
            rows = work.tile([P, PACK, N], BF16, tag="weighted", bufs=3, align_bytes=64)
            for t in range(PACK):
                nc.scalar.activation(
                    out=rows[:, t, :], in_=squares[g, h][:, t, :], func=ACT.Copy, scale=norm[:, g, t : t + 1]
                )
            weighted[g, h] = rows

        def interleave(g, h):
            grouped = []
            for u in range(2):
                part = work.tile([P, PART, PACK], BF16, tag="grouped", bufs=4, align_bytes=64)
                nc.vector.tensor_copy(
                    out=part[:].rearrange("p (j i) t -> p j t i", i=4),
                    in_=weighted[g, h][:, :, span(u, PART)].rearrange("p t (j i) -> p j t i", i=4),
                )
                grouped.append(part)
            quantize(g, h, grouped)

        sums = {}

        def map_passes(h, i, cols, groups):
            key = (h, i, cols.start)
            width = cols.stop - cols.start
            if key not in sums:
                bank = psum.tile([P, width], F32, tag="bank")
                sums[key] = bank
            voxels = span(i % 2, P)
            for g in groups:
                nc.tensor.matmul_mx(
                    out=sums[key][:],
                    lhsT=e_words[g, h, i // 2][:, voxels].bitcast(FP8X4),
                    lhsT_scale=e_scales[g, h, i // 2][:, voxels],
                    rhs=m_words[g][:, cols].bitcast(FP8X4),
                    rhs_scale=m_scales[4 * g :, cols],
                    start=(g == 0),
                    stop=(g == GROUPS - 1),
                )

        out_rows = out.rearrange("(h m i) r -> h i m r", m=P, i=PACK)

        def finish(h, i, cols):
            res = work.tile([P, cols.stop - cols.start], F32, tag="result", bufs=8)
            nc.vector.scalar_tensor_tensor(
                out=res[:],
                in0=sums[h, i, cols.start][:],
                scalar=energy[:, h, i : i + 1],
                in1=base_all[:, cols],
                op0=ALU.mult,
                op1=ALU.add,
            )
            nc.sync.dma_start(out=out_rows[h, i, :, cols], in_=res[:])

        for t in range(PACK):
            sort_atoms(0, t, 1)
        correlate(0, 0)
        for g in range(1, GROUPS):
            sort_atoms(g, 0, PACK)
            correlate(g, 0)
        for g in range(GROUPS):
            correlate(g, 1)
            weigh_on_vector(g, 0)
        weigh_on_vector(0, 1)
        for g in range(1, GROUPS):
            weigh_on_scalar(g, 1)

        tiles = [(i, span(r, N)) for i in range(PACK) for r in range(R_HALVES)]
        early, late = tiles[:4], tiles[4:]
        everything = list(range(GROUPS))
        for g in everything:
            for i, cols in early:
                map_passes(0, i, cols, [g])
        for i, cols in late:
            map_passes(0, i, cols, everything)
        interleave(1, 1)
        for i, cols in early[:2]:
            finish(0, i, cols)
        interleave(2, 1)
        for i, cols in early[2:]:
            finish(0, i, cols)
        interleave(3, 1)
        for i, cols in early:
            map_passes(1, i, cols, everything[:-1])
        for i, cols in early:
            map_passes(1, i, cols, everything[-1:])
        for i, cols in late:
            finish(0, i, cols)
        last = late[:-1] + [(PACK - 1, span(j, PART)) for j in (2, 3)]
        for i, cols in last[:-1]:
            map_passes(1, i, cols, everything)
        finish(1, *early[0])
        map_passes(1, *last[-1], everything)
        for i, cols in early[1:] + last:
            finish(1, i, cols)
